import numpy as np, ml_dtypes
CORES = [0,1,2,3,4,5,6,7,8,9,10,11,12,13,14,15]
N = 16
def setup_inputs(rng):
    return {"x": rng.standard_normal((N, 128, 16), dtype=np.float32).astype(ml_dtypes.bfloat16)}
def reference(x):
    g = np.concatenate(list(x), axis=1).astype(np.float32)
    return {"y": np.broadcast_to(g, (N,) + g.shape)}

@@ -1,0 +1,60 @@
+import concourse.bass as bass
+
+SCRATCH = {
+    "land": ("sbuf", [128, 256], "bfloat16"),
+    "wide": ("sbuf", [128, 256], "float32"),
+}
+SEMAPHORES = ["loaded", "sent", "near", "far", "widened", "stored"]
+
+W = 16
+CHIPW = 8 * W
+GATES = (2, 3, 6, 7)
+
+
+def dst_id(topo, c):
+    rid, pid, se = topo.addr(c)
+    return bass.DstId(rid=rid, pnc=pid)
+
+
+def rank_program(g, core, T, topo):
+    rank = T.rank_of(core)
+    if rank is None:
+        return
+    ch, k = divmod(core, 8)
+    base = 8 * ch
+    other = 8 * (ch ^ 1)
+    S = T.sem
+    mine = T.land[:, W * rank:W * (rank + 1)]
+
+    g.sync.dma_start(mine, T.x[:]).then_inc(S.loaded, 16)
+    g.wait_ge(S.loaded, 16)
+
+    peers = [base + j for j in range(8) if j != k]
+    g.remote_dma_fused(
+        [bass.RemoteDMATransfer(
+            dst_ids=[dst_id(topo, p) for p in peers], dma_engine_mask=0xFFFF, remote_sem=S.near,
+            srcs=[mine], dsts=[mine for p in peers])],
+        local_sem=S.sent)
+    sent = 16
+
+    if k in GATES:
+        g.wait_ge(S.near, 7 * 16)
+        block = T.land[:, CHIPW * ch:CHIPW * (ch + 1)]
+        first = {2: 0, 3: 2, 6: 4, 7: 6}[k]
+        tgt = [other + first, other + first + 1]
+        g.remote_dma_fused(
+            [bass.RemoteDMATransfer(
+                dst_ids=[dst_id(topo, p) for p in tgt], dma_engine_mask=0x00FF, remote_sem=S.far,
+                srcs=[block], dsts=[block for p in tgt])],
+            local_sem=S.sent)
+        sent += 8
+    g.wait_ge(S.sent, sent)
+
+    v = g.vector
+    v.wait_ge(S.loaded, 16)
+    v.wait_ge(S.near, 7 * 16)
+    v.wait_ge(S.far, 8)
+    v.tensor_copy(T.wide[:], T.land[:]).then_inc(S.widened, 1)
+    g.sync.wait_ge(S.widened, 1)
+    g.sync.dma_start(T.y[:], T.wide[:]).then_inc(S.stored, 16)
+    g.sync.wait_ge(S.stored, 16)

@@ -25,6 +25,8 @@ def rank_program(g, core, T, topo):
     other = 8 * (ch ^ 1)
     S = T.sem
     mine = T.land[:, W * rank:W * (rank + 1)]
+    lo, hi = CHIPW * ch, CHIPW * (ch + 1)
+    flo, fhi = CHIPW * (ch ^ 1), CHIPW * ((ch ^ 1) + 1)
 
     g.sync.dma_start(mine, T.x[:]).then_inc(S.loaded, 16)
     g.wait_ge(S.loaded, 16)
@@ -39,7 +41,7 @@ def rank_program(g, core, T, topo):
 
     if k in GATES:
         g.wait_ge(S.near, 7 * 16)
-        block = T.land[:, CHIPW * ch:CHIPW * (ch + 1)]
+        block = T.land[:, lo:hi]
         first = {2: 0, 3: 2, 6: 4, 7: 6}[k]
         tgt = [other + first, other + first + 1]
         g.remote_dma_fused(
@@ -53,8 +55,11 @@ def rank_program(g, core, T, topo):
     v = g.vector
     v.wait_ge(S.loaded, 16)
     v.wait_ge(S.near, 7 * 16)
+    v.tensor_copy(T.wide[:, lo:hi], T.land[:, lo:hi]).then_inc(S.widened, 1)
     v.wait_ge(S.far, 8)
-    v.tensor_copy(T.wide[:], T.land[:]).then_inc(S.widened, 1)
+    v.tensor_copy(T.wide[:, flo:fhi], T.land[:, flo:fhi]).then_inc(S.widened, 1)
     g.sync.wait_ge(S.widened, 1)
-    g.sync.dma_start(T.y[:], T.wide[:]).then_inc(S.stored, 16)
-    g.sync.wait_ge(S.stored, 16)
+    g.sync.dma_start(T.y[:, lo:hi], T.wide[:, lo:hi]).then_inc(S.stored, 16)
+    g.sync.wait_ge(S.widened, 2)
+    g.sync.dma_start(T.y[:, flo:fhi], T.wide[:, flo:fhi]).then_inc(S.stored, 16)
+    g.sync.wait_ge(S.stored, 32)

@@ -16,6 +16,10 @@ def dst_id(topo, c):
     return bass.DstId(rid=rid, pnc=pid)
 
 
+def engines(mask):
+    return bin(mask).count("1")
+
+
 def rank_program(g, core, T, topo):
     rank = T.rank_of(core)
     if rank is None:
@@ -27,34 +31,37 @@ def rank_program(g, core, T, topo):
     mine = T.land[:, W * rank:W * (rank + 1)]
     lo, hi = CHIPW * ch, CHIPW * (ch + 1)
     flo, fhi = CHIPW * (ch ^ 1), CHIPW * ((ch ^ 1) + 1)
+    gate = k in GATES
+
+    def spread(ap, targets, mask, sem):
+        g.remote_dma_fused(
+            [bass.RemoteDMATransfer(
+                dst_ids=[dst_id(topo, p) for p in targets], dma_engine_mask=mask, remote_sem=sem,
+                srcs=[ap], dsts=[ap for p in targets])],
+            local_sem=S.sent)
+        return engines(mask)
+
+    if gate:
+        near_all = 7 * 16
+    else:
+        near_all = 3 * 16 + 4 * 8
 
     g.sync.dma_start(mine, T.x[:]).then_inc(S.loaded, 16)
     g.wait_ge(S.loaded, 16)
 
-    peers = [base + j for j in range(8) if j != k]
-    g.remote_dma_fused(
-        [bass.RemoteDMATransfer(
-            dst_ids=[dst_id(topo, p) for p in peers], dma_engine_mask=0xFFFF, remote_sem=S.near,
-            srcs=[mine], dsts=[mine for p in peers])],
-        local_sem=S.sent)
-    sent = 16
+    sent = spread(mine, [base + j for j in GATES if j != k], 0xFFFF, S.near)
+    sent += spread(mine, [base + j for j in range(8) if j not in GATES and j != k],
+                   0xFF00 if gate else 0xFFFF, S.near)
 
-    if k in GATES:
-        g.wait_ge(S.near, 7 * 16)
-        block = T.land[:, lo:hi]
+    if gate:
+        g.wait_ge(S.near, near_all)
         first = {2: 0, 3: 2, 6: 4, 7: 6}[k]
-        tgt = [other + first, other + first + 1]
-        g.remote_dma_fused(
-            [bass.RemoteDMATransfer(
-                dst_ids=[dst_id(topo, p) for p in tgt], dma_engine_mask=0x00FF, remote_sem=S.far,
-                srcs=[block], dsts=[block for p in tgt])],
-            local_sem=S.sent)
-        sent += 8
+        sent += spread(T.land[:, lo:hi], [other + first, other + first + 1], 0x00FF, S.far)
     g.wait_ge(S.sent, sent)
 
     v = g.vector
     v.wait_ge(S.loaded, 16)
-    v.wait_ge(S.near, 7 * 16)
+    v.wait_ge(S.near, near_all)
     v.tensor_copy(T.wide[:, lo:hi], T.land[:, lo:hi]).then_inc(S.widened, 1)
     v.wait_ge(S.far, 8)
     v.tensor_copy(T.wide[:, flo:fhi], T.land[:, flo:fhi]).then_inc(S.widened, 1)

@@ -8,7 +8,7 @@ SEMAPHORES = ["loaded", "sent", "near", "far", "widened", "stored"]
 
 W = 16
 CHIPW = 8 * W
-GATES = (2, 3, 6, 7)
+GATES = (2, 6, 3, 7)
 
 
 def dst_id(topo, c):

import concourse.bass as bass

SCRATCH = {
    "land": ("sbuf", [128, 256], "bfloat16"),
    "wide": ("sbuf", [128, 256], "float32"),
}
SEMAPHORES = ["loaded", "sent", "near", "far", "widened", "stored"]

W = 16
CHIPW = 8 * W
GATES = (2, 6, 3, 7)


def dst_id(topo, c):
    rid, pid, se = topo.addr(c)
    return bass.DstId(rid=rid, pnc=pid)


def engines(mask):
    return bin(mask).count("1")


def rank_program(g, core, T, topo):
    rank = T.rank_of(core)
    if rank is None:
        return
    ch, k = divmod(core, 8)
    base = 8 * ch
    other = 8 * (ch ^ 1)
    S = T.sem
    mine = T.land[:, W * rank:W * (rank + 1)]
    lo, hi = CHIPW * ch, CHIPW * (ch + 1)
    flo, fhi = CHIPW * (ch ^ 1), CHIPW * ((ch ^ 1) + 1)
    gate = k in GATES

    def spread(ap, targets, mask, sem):
        g.remote_dma_fused(
            [bass.RemoteDMATransfer(
                dst_ids=[dst_id(topo, p) for p in targets], dma_engine_mask=mask, remote_sem=sem,
                srcs=[ap], dsts=[ap for p in targets])],
            local_sem=S.sent)
        return engines(mask)

    if gate:
        near_all = 7 * 16
    else:
        near_all = 3 * 16 + 4 * 8

    g.sync.dma_start(mine, T.x[:]).then_inc(S.loaded, 16)
    g.wait_ge(S.loaded, 16)

    sent = spread(mine, [base + j for j in GATES if j != k], 0xFFFF, S.near)
    sent += spread(mine, [base + j for j in range(8) if j not in GATES and j != k],
                   0xFF00 if gate else 0xFFFF, S.near)

    if gate:
        g.wait_ge(S.near, near_all)
        first = {2: 0, 3: 2, 6: 4, 7: 6}[k]
        sent += spread(T.land[:, lo:hi], [other + first, other + first + 1], 0x00FF, S.far)
    g.wait_ge(S.sent, sent)

    v = g.vector
    v.wait_ge(S.loaded, 16)
    v.wait_ge(S.near, near_all)
    v.tensor_copy(T.wide[:, lo:hi], T.land[:, lo:hi]).then_inc(S.widened, 1)
    v.wait_ge(S.far, 8)
    v.tensor_copy(T.wide[:, flo:fhi], T.land[:, flo:fhi]).then_inc(S.widened, 1)
    g.sync.wait_ge(S.widened, 1)
    g.sync.dma_start(T.y[:, lo:hi], T.wide[:, lo:hi]).then_inc(S.stored, 16)
    g.sync.wait_ge(S.widened, 2)
    g.sync.dma_start(T.y[:, flo:fhi], T.wide[:, flo:fhi]).then_inc(S.stored, 16)
    g.sync.wait_ge(S.stored, 32)
